import numpy as np, ml_dtypes
CORES = [8,80,112,136,208,240,264,336,368,392,464,496]
N = 12
DEG, TK = 2, 256
MASK = [[3,0],[3,1],[3,2],[3,0],[3,4],[3,5],[3,6],[3,7],[3,8],[3,9],[3,10],[3,11]]
def setup_inputs(rng):
    return {"x": rng.standard_normal((N, 128, TK), dtype=np.float32).astype(ml_dtypes.bfloat16), "w": rng.standard_normal((N, 128, DEG * 128), dtype=np.float32).astype(ml_dtypes.bfloat16)}
def setup_inputs_big(rng):
    d = setup_inputs(rng)
    for k in ("x", "w"): d[k] = (d[k].astype(np.float32) * 1024.0).astype(d[k].dtype)
    return d
def setup_inputs_small(rng):
    d = setup_inputs(rng)
    for k in ("x", "w"): d[k] = (d[k].astype(np.float32) * (1 / 1024.0)).astype(d[k].dtype)
    return d
def setup_inputs_apart(rng):
    d = setup_inputs(rng)
    f = (10.0 ** rng.permutation(np.linspace(-1.5, 1.5, N))).astype(np.float32).reshape(N, 1, 1)
    for k in ("x", "w"): d[k] = (d[k].astype(np.float32) * f).astype(d[k].dtype)
    return d
def reference(x, w):
    X, W = x.astype(np.float64), w.astype(np.float64)
    y = np.zeros((N, 128, TK))
    for r in range(N):
        for i, j in enumerate(MASK[r]):
            y[r] += W[r][:, 128 * i:128 * i + 128].T @ X[j]
    return {"y": y.astype(ml_dtypes.bfloat16 if x.dtype != np.float64 else np.float64)}

from concourse.bass import DstId, RemoteDMATransfer

P, TK, DEG = 128, 256, 2
NE = 8

SCRATCH = {
    "xin": ("sbuf", [P, DEG * TK], "bfloat16"),
    "ws": ("sbuf", [P, DEG * P], "bfloat16"),
    "ys": ("sbuf", [P, TK], "bfloat16"),
    "xd": ("dram", [P, TK], "bfloat16"),
    "ps": ("psum", [P, TK], "float32"),
}
SEMAPHORES = ["ldd", "ldx", "ldw", "arr0", "arr1", "sent", "mm", "cp", "st"]

XD = -1
_CACHE = {}


def _take(mask, n):
    out, k, b = 0, 0, 0
    while k < n and (mask >> b):
        if (mask >> b) & 1:
            out |= 1 << b
            k += 1
        b += 1
    return out


def _count(mask):
    return bin(mask).count("1")


def _plan(T, topo):
    cores, tab = list(T.cores), T.tables["MASK"]
    n = len(cores)
    world = range((topo.host(max(cores)) + 1) * topo.CORES_PER_HOST)
    steps, arrive, stage, busy = {}, {}, set(), set(cores)
    owners = [j for j in range(n) if any(j in tab[r] for r in range(n) if r != j)]

    def twin(h, s):
        return [c for c in world if topo.host(c) == h and topo.chip(c) == topo.chip(s)]

    def common(src, dsts, avoid=0):
        m = ~avoid
        for d in dsts:
            m &= topo.mask(src, d)
        return _take(m, NE)

    def add(core, depth, wait, src, transfers):
        steps.setdefault(core, []).append((depth, wait, src, transfers))
        for eng, sl, dsts in transfers:
            for d, _ in dsts:
                arrive[(d, sl)] = arrive.get((d, sl), 0) + _count(eng)

    for j in owners:
        s = cores[j]
        slot = {cores[r]: tab[r].index(j) for r in range(n) if r != j and j in tab[r]}
        direct = [d for d in slot if topo.may_write(s, d)]
        rest = [d for d in slot if d not in direct]
        fwd = {}
        for d in list(rest):
            c = [f for f in direct if topo.may_write(f, d)]
            if c:
                f = min(c, key=lambda f: (len(fwd.get(f, [])), T.rank_of(f) not in owners, f))
                fwd.setdefault(f, []).append(d)
                rest.remove(d)
        lanes = {"on": [], "off": []}
        for h in sorted(set(topo.host(d) for d in rest)):
            grp = [d for d in rest if topo.host(d) == h]
            here = topo.rack(h) == topo.rack(topo.host(s))

            def able(cs):
                cs = [c for c in cs if c not in busy and topo.may_write(s, c) and all(topo.may_write(c, d) for d in grp)]
                return sorted(cs, key=lambda c: (topo.die(c) != topo.die(s), c))

            near = able(twin(topo.host(s), s))
            if near and (h == topo.host(s) or not here):
                lanes["on"].append((not here, grp, near))
            else:
                hs = sorted(set(topo.host(c) for c in world),
                            key=lambda k: (k != h, topo.rack(k) != topo.rack(h), k))
                far = [able(twin(k, s)) for k in hs if k != topo.host(s)]
                far = [f for f in far if f][0]
                lanes["off"].append((topo.rack(topo.host(far[0])) == topo.rack(topo.host(s)), grp, far))
        feeds = []
        for name in ("off", "on"):
            relays = []
            for k, (_, grp, able_cores) in enumerate(sorted(lanes[name], key=lambda e: e[0])):
                free = [c for c in able_cores if c not in busy]
                parts = [grp] if k == 0 else [[d] for d in grp]
                for i, part in enumerate(parts):
                    relays.append((free[i], part))
                    busy.add(free[i])
            if relays:
                feeds.append(relays)
        if feeds:
            stage.add(s)
            used, transfers = 0, []
            for relays in feeds:
                eng = common(s, [c for c, _ in relays], used)
                used |= eng
                transfers.append((eng, 0, [(c, XD) for c, _ in relays]))
            add(s, 0, ("ldd", 16), XD, transfers)
            for relays in feeds:
                for c, part in relays:
                    for sl in sorted(set(slot[d] for d in part)):
                        ds = [d for d in part if slot[d] == sl]
                        add(c, 1, ("arr0", arrive[(c, 0)]), XD, [(common(c, ds), sl, [(d, sl) for d in ds])])
        elif j not in tab[j]:
            stage.add(s)
        src = XD if s in stage else tab[j].index(j)
        wait = ("ldd", 16) if s in stage else ("ldx", 16)
        direct.sort(key=lambda d: (d not in fwd, d))
        for sl in sorted(set(slot[d] for d in direct)):
            ds = [d for d in direct if slot[d] == sl]
            add(s, 0, wait, src, [(common(s, ds), sl, [(d, sl) for d in ds])])
        for f, ds in fwd.items():
            for sl in sorted(set(slot[d] for d in ds)):
                dd = [d for d in ds if slot[d] == sl]
                add(f, 1, ("arr%d" % slot[f], arrive[(f, slot[f])]), slot[f], [(common(f, dd), sl, [(d, sl) for d in dd])])
    for c in steps:
        steps[c].sort(key=lambda e: e[0])
    return {"steps": steps, "arrive": arrive, "stage": stage}


def rank_program(g, core, T, topo):
    if "plan" not in _CACHE:
        _CACHE["plan"] = _plan(T, topo)
    plan = _CACHE["plan"]
    steps, arrive = plan["steps"].get(core, []), plan["arrive"]
    rank = T.rank_of(core)
    if rank is None and not steps:
        return
    S = T.sem

    def place(where):
        return T.xd[:] if where == XD else T.xin[:, where * TK:(where + 1) * TK]

    if rank is not None:
        mine = T.tables["MASK"][rank]
        own = mine.index(rank) if rank in mine else None
        if core in plan["stage"]:
            g.sync.dma_start(T.xd[:], T.x[:]).then_inc(S.ldd, 16)
            wq = g.sync
        else:
            wq = g.scalar
        if own is not None:
            g.sync.dma_start(place(own), T.x[:]).then_inc(S.ldx, 16)
        wq.dma_start(T.ws[:], T.w[:]).then_inc(S.ldw, 16)

    total, waited = 0, None
    for _, (sem, cnt), src, transfers in steps:
        if (sem, cnt) != waited:
            g.wait_ge(S[sem], cnt)
            waited = (sem, cnt)
        trs = []
        for eng, sl, dsts in transfers:
            ids = []
            for d, _ in dsts:
                rid, pid = topo.addr(d, core)
                ids.append(DstId(rid=rid, pnc=pid))
            trs.append(RemoteDMATransfer(dst_ids=ids, dma_engine_mask=eng, remote_sem=S["arr%d" % sl],
                                         srcs=[place(src)], dsts=[place(w) for _, w in dsts], alu_op=0))
            total += _count(eng)
        g.remote_dma_fused(trs, local_sem=S.sent)
    if total:
        g.wait_ge(S.sent, total)
    if rank is None:
        return

    order = sorted(range(len(mine)), key=lambda i: (mine[i] != rank, i))
    g.tensor.wait_ge(S.ldw, 16)
    seen = set()
    for k, i in enumerate(order):
        sl = mine.index(mine[i])
        if sl not in seen:
            seen.add(sl)
            if mine[i] == rank:
                g.tensor.wait_ge(S.ldx, 16)
            else:
                g.tensor.wait_ge(S["arr%d" % sl], arrive[(core, sl)])
        mm = g.tensor.matmul(T.ps[:], T.ws[:, i * P:(i + 1) * P], place(sl), start=(k == 0), stop=(k == len(order) - 1))
    mm.then_inc(S.mm, 1)
    g.vector.wait_ge(S.mm, 1)
    g.vector.tensor_copy(T.ys[:], T.ps[:]).then_inc(S.cp, 1)
    g.sync.wait_ge(S.cp, 1)
    g.sync.dma_start(T.y[:], T.ys[:]).then_inc(S.st, 16)
    g.sync.wait_ge(S.st, 16)
